import numpy as np, ml_dtypes
CORES = [51,54,179,182]
N = 4
import mx_ref
NC, G, S2 = 128, 4, 1
C = np.float32(0.019)
CNT = [[0,92,36,0],[0,0,24,104],[104,0,0,24],[24,36,68,0]]
OFF = [[sum(c[:e]) for e in range(N + 1)] for c in CNT]
BF = ml_dtypes.bfloat16
def cut(t, i, w=512):
    return t[:, w * i:w * i + w]
def tile(rs):
    return np.stack(rs, axis=2).reshape(128, -1).astype(BF)
def layer(w, X):
    out = []
    for i in range(G):
        for t in range(len(X)):
            p = mx_ref.matmul(mx_ref.quantize(cut(w, len(X) * i + t)), X[t])
            z = p if t == 0 else z + p
        out.append(z)
    return out
def act(Z):
    return [np.maximum(z, 0) * C for z in Z]
def setup_inputs(rng):
    def f(*shape):
        return mx_ref.flush((rng.standard_normal(shape, dtype=np.float32) * np.exp2(rng.integers(-2, 3, shape[:-1] + (1,)))).astype(BF))
    gt = (0.125 + 0.875 * rng.random((N, 2, NC))).astype(BF)
    return {"gt": gt, "x": f(N, 128, 4 * NC), "w1": f(N, 128, G * 512), "w2": f(N, 128, 512)}
def setup_inputs_blocks(rng):
    d = setup_inputs(rng)
    for k in ("x", "w1", "w2"): d[k] = mx_ref.spread(d[k], rng, 4)
    return d
def setup_inputs_wide(rng):
    d = setup_inputs(rng)
    for k in ("x", "w1", "w2"): d[k] = mx_ref.flush((d[k].astype(np.float32) * np.exp2(rng.integers(-8, 9, (N, 1, 1))).astype(np.float32)).astype(BF))
    return d
def setup_inputs_zeros(rng):
    d = setup_inputs(rng); v = d["x"].reshape(N, 128, -1, 4).copy()
    v[np.broadcast_to((rng.random((N, 1, v.shape[2], 1)) < 0.33), v.shape)] = 0
    d["x"] = v.reshape(d["x"].shape)
    return d
def reference(gt, x, w1, w2):
    y = np.zeros((N, 128, NC), np.float32); g = gt.astype(np.float32)
    for e in range(N):
        f = (e - S2) % N
        t = np.concatenate([x[j][:, 4 * OFF[j][k]:4 * OFF[j][k + 1]] for k in (e, f) for j in range(N)], axis=1)
        p = mx_ref.matmul(mx_ref.quantize(w2[e]), mx_ref.quantize(tile(act(layer(w1[e], [mx_ref.quantize(t)])))))
        c = 0
        for i, k in enumerate((e, f)):
            for j in range(N):
                a, b = OFF[j][k], OFF[j][k + 1]
                y[j][:, a:b] = y[j][:, a:b] + p[:, c:c + b - a] * g[j, i, a:b]; c += b - a
    return {"y": y}

@@ -1,0 +1,240 @@
+from concourse.mybir import dt, AluOpType, ActivationFunctionType
+
+N = 4
+NC = 128
+G = 4
+STEP = 1
+C = 0.019
+LEAST = 128
+XW = 512
+EW = 192
+
+SCRATCH = {
+    "xb": ("sbuf", [128, 4 * NC], "bfloat16"),
+    "w1b": ("sbuf", [128, G * 512], "bfloat16"),
+    "w2b": ("sbuf", [128, 512], "bfloat16"),
+    "w1c": ("sbuf", [128, G * 128], "float8_e4m3fn_x4"),
+    "w1s": ("sbuf", [128, G * 128], "uint8"),
+    "w2c": ("sbuf", [128, 128], "float8_e4m3fn_x4"),
+    "w2s": ("sbuf", [128, 128], "uint8"),
+    "xc": ("sbuf", [128, XW], "float8_e4m3fn_x4"),
+    "xs": ("sbuf", [128, XW], "uint8"),
+    "hE": ("sbuf", [128, 4 * EW], "bfloat16"),
+    "hL": ("sbuf", [128, 4 * EW], "bfloat16"),
+    "hcE": ("sbuf", [128, EW], "float8_e4m3fn_x4"),
+    "hcL": ("sbuf", [128, EW], "float8_e4m3fn_x4"),
+    "hsE": ("sbuf", [128, EW], "uint8"),
+    "hsL": ("sbuf", [128, EW], "uint8"),
+    "pE": ("sbuf", [128, EW], "float32"),
+    "pL": ("sbuf", [128, EW], "float32"),
+    "ra": ("sbuf", [128, NC], "float32"),
+    "rb": ("sbuf", [128, NC], "float32"),
+    "grow": ("sbuf", [1, 2 * NC], "bfloat16"),
+    "gall": ("sbuf", [128, 2 * NC], "bfloat16"),
+    "gb": ("sbuf", [128, NC], "bfloat16"),
+    "ta": ("sbuf", [128, NC], "float32"),
+    "tb": ("sbuf", [128, NC], "float32"),
+    "yb": ("sbuf", [128, NC], "float32"),
+    "ps": ("psum", [128, 512 * 8], "float32"),
+}
+SEMAPHORES = (["ldx", "ldw1a", "ldw1b", "ldw2", "ldg", "qx", "qw1a", "qw1b", "qw2", "gdone", "sent",
+               "x_near", "x_far", "x_on", "r_near", "r_late", "gbs", "tas", "tbs", "ys", "sty"]
+              + ["%s%s" % (n, b) for b in "EL" for n in ("z0", "z1", "z2", "z3", "as", "av", "hq", "p", "ev")])
+
+
+def run_of(cnt, j, e):
+    a = b = None
+    at = 0
+    for k in range(N):
+        w = cnt[j][k]
+        if w and (k == e or (k + STEP) % N == e):
+            if a is None:
+                a = at
+            elif b != at:
+                raise ValueError("not one run")
+            b = at + w
+        at += w
+    return (0, 0) if a is None else (a, b)
+
+
+def peers_of(T, topo, e):
+    c = T.cores[e]
+    out = {}
+    for j in range(N):
+        d = T.cores[j]
+        if j == e:
+            continue
+        if (topo.host(c), topo.chip(c)) == (topo.host(d), topo.chip(d)):
+            out["on"] = j
+        elif topo.die(c) == topo.die(d):
+            out["near"] = j
+        else:
+            out["far"] = j
+    return out
+
+
+def plan_of(T, topo, e):
+    cnt = T.tables["CNT"]
+    p = peers_of(T, topo, e)
+    wide = {}
+    for way in p:
+        a, b = run_of(cnt, p[way], e)
+        wide[way] = b - a
+    a0, b0 = run_of(cnt, e, e)
+    own = b0 - a0
+    if own and b0 != NC:
+        raise ValueError("own run must end the tile")
+    if own + wide["on"] + wide["far"] <= LEAST:
+        order, early, late = ("on", "far", "near"), ("near",), ("far", "on")
+    else:
+        if own:
+            raise ValueError("own run has no batch")
+        order, early, late = ("on", "near", "far"), ("on", "near"), ("far",)
+    at, lo = {}, NC
+    for way in order:
+        at[p[way]] = lo
+        lo += wide[way]
+    ends = {}
+    for name, ways in (("E", early), ("L", late)):
+        s = min(at[p[w]] for w in ways)
+        t = max(at[p[w]] + wide[w] for w in ways)
+        if name == "L":
+            s -= own
+        if t - s < LEAST:
+            s = t - LEAST
+        ends[name] = (s, t)
+    return {"peers": p, "at": at, "batch": ends, "ways": {"E": early, "L": late}}
+
+
+def rank_program(g, core, T, topo):
+    rank = T.rank_of(core)
+    if rank is None:
+        return
+    sem = T.sem
+    cnt = T.tables["CNT"]
+    me = plan_of(T, topo, rank)
+    peers = me["peers"]
+    off_mask = topo.mask(core, T.cores[peers["near"]])
+    masks = {"near": off_mask, "far": topo.mask(core, T.cores[peers["far"]]),
+             "on": topo.mask(core, T.cores[peers["on"]]) & ~off_mask}
+    eng = {w: bin(masks[w]).count("1") for w in masks}
+    sent = [0]
+
+    def send(way, out_ap, in_ap, remote_sem):
+        rid, pid = topo.addr(T.cores[peers[way]], core)
+        g.remote_dma(out_ap, in_ap, remote_sem, sem["sent"], pid, rid, masks[way])
+        sent[0] += eng[way]
+
+    g.sync.dma_start(T.xb[:], T.x[:]).then_inc(sem["ldx"], 16)
+    g.sync.dma_start(T.w1b[:, 0:1024], T.w1[:, 0:1024]).then_inc(sem["ldw1a"], 16)
+    g.sync.dma_start(T.w1b[:, 1024:2048], T.w1[:, 1024:2048]).then_inc(sem["ldw1b"], 16)
+    g.sync.dma_start(T.w2b[:], T.w2[:]).then_inc(sem["ldw2"], 16)
+    g.scalar.dma_start(T.grow[:], T.gt[:]).then_inc(sem["ldg"], 16)
+
+    v = g.vector
+    v.wait_ge(sem["ldx"], 16)
+    v.quantize_mx(T.xc[:, 0:NC], T.xs[:, 0:NC], T.xb[:]).then_inc(sem["qx"], 1)
+    v.wait_ge(sem["ldw1a"], 16)
+    v.quantize_mx(T.w1c[:, 0:256], T.w1s[:, 0:256], T.w1b[:, 0:1024]).then_inc(sem["qw1a"], 1)
+    v.wait_ge(sem["ldw1b"], 16)
+    v.quantize_mx(T.w1c[:, 256:512], T.w1s[:, 256:512], T.w1b[:, 1024:2048]).then_inc(sem["qw1b"], 1)
+    v.wait_ge(sem["ldw2"], 16)
+    v.quantize_mx(T.w2c[:], T.w2s[:], T.w2b[:]).then_inc(sem["qw2"], 1)
+
+    g.wait_ge(sem["qx"], 1)
+    for way in ("near", "far", "on"):
+        e = peers[way]
+        a, b = run_of(cnt, rank, e)
+        d = plan_of(T, topo, e)["at"][rank]
+        send(way, T.xc[:, d:d + b - a].bitcast(dt.uint8), T.xc[:, a:b].bitcast(dt.uint8), sem["x_" + way])
+        send(way, T.xs[:, d:d + b - a], T.xs[:, a:b], sem["x_" + way])
+
+    g.wait_ge(sem["ldg"], 16)
+    g.partition_broadcast(T.gall[:], T.grow[:], 128).then_inc(sem["gdone"], 1)
+
+    t = g.tensor
+    banks = {"E": (0, 1, 2, 3, 4), "L": (5, 6, 7, 0, 1)}
+
+    def bank(b, k, lo, hi):
+        return T.ps[:, 512 * banks[b][k] + lo:512 * banks[b][k] + hi]
+
+    def back(b, way):
+        a, z = run_of(cnt, peers[way], rank)
+        s = me["at"][peers[way]] - me["batch"][b][0]
+        return s, s + z - a, a, z
+
+    for b in "EL":
+        ways = me["ways"][b]
+        lo, hi = me["batch"][b]
+        n = hi - lo
+        h, hc, hs, p = T["h" + b], T["hc" + b], T["hs" + b], T["p" + b]
+        t.wait_ge(sem["qw1a" if b == "E" else "qx"], 1)
+        for way in ways:
+            t.wait_ge(sem["x_" + way], 2 * eng[way])
+        for k in range(G):
+            if b == "E" and k == 2:
+                t.wait_ge(sem["qw1b"], 1)
+            w = slice(128 * k, 128 * k + 128)
+            t.matmul_mx(bank(b, k, 0, n), T.w1c[:, w], T.w1s[:, w], T.xc[:, lo:hi], T.xs[:, lo:hi],
+                        True, True).then_inc(sem["z%d%s" % (k, b)], 1)
+        for k in (0, 2):
+            g.scalar.wait_ge(sem["z%d%s" % (k, b)], 1)
+            g.scalar.activation(h[:, k:4 * n:4], bank(b, k, 0, n), ActivationFunctionType.Relu,
+                                scale=C).then_inc(sem["as" + b], 1)
+        for k in (1, 3):
+            v.wait_ge(sem["z%d%s" % (k, b)], 1)
+            v.tensor_scalar(h[:, k:4 * n:4], bank(b, k, 0, n), 0.0, C, AluOpType.max,
+                            AluOpType.mult).then_inc(sem["av" + b], 1)
+        v.wait_ge(sem["as" + b], 2)
+        v.wait_ge(sem["av" + b], 2)
+        v.quantize_mx(hc[:, 0:n], hs[:, 0:n], h[:, 0:4 * n]).then_inc(sem["hq" + b], 1)
+        if b == "E":
+            t.wait_ge(sem["qw2"], 1)
+        t.wait_ge(sem["hq" + b], 1)
+        t.matmul_mx(bank(b, 4, 0, n), T.w2c[:], T.w2s[:], hc[:, 0:n], hs[:, 0:n], True, True).then_inc(sem["p" + b], 1)
+        pieces = [back(b, w) for w in ways]
+        s0, s1 = min(q[0] for q in pieces), max(q[1] for q in pieces)
+        if b == "E":
+            g.scalar.wait_ge(sem["p" + b], 1)
+            g.scalar.activation(p[:, s0:s1], bank(b, 4, s0, s1), ActivationFunctionType.Copy).then_inc(sem["ev" + b], 1)
+        else:
+            v.wait_ge(sem["p" + b], 1)
+            v.tensor_copy(p[:, s0:s1], bank(b, 4, s0, s1)).then_inc(sem["ev" + b], 1)
+        g.wait_ge(sem["ev" + b], 1)
+        for way in sorted(ways, key=lambda w: w == "on"):
+            s, z, a, c = back(b, way)
+            send(way, T["ra" if way == "near" else "rb"][:, a:c], p[:, s:z], sem["r_near" if way == "near" else "r_late"])
+
+    segs, at = [], 0
+    for k in range(N):
+        w = cnt[rank][k]
+        if w:
+            pair = (k, (k + STEP) % N)
+            mine = peers["near"] if peers["near"] in pair else rank
+            if mine not in pair:
+                raise ValueError("no near or own expert")
+            segs.append((at, at + w, 0 if pair[0] == mine else 1, mine == rank))
+        at += w
+    v.wait_ge(sem["gdone"], 1)
+    for a, z, row, _own in segs:
+        o = NC * (1 - row)
+        v.tensor_copy(T.gb[:, a:z], T.gall[:, o + a:o + z]).then_inc(sem["gbs"], 1)
+    for own_turn in (True, False):
+        if not own_turn:
+            v.wait_ge(sem["r_near"], eng["near"])
+        for a, z, row, is_own in segs:
+            if is_own == own_turn:
+                lo = me["batch"]["L"][0]
+                src = bank("L", 4, a - lo, z - lo) if is_own else T.ra[:, a:z]
+                v.tensor_tensor(T.ta[:, a:z], src, T.gall[:, NC * row + a:NC * row + z],
+                                AluOpType.mult).then_inc(sem["tas"], 1)
+    v.wait_ge(sem["gbs"], len(segs))
+    v.wait_ge(sem["tas"], len(segs))
+    v.wait_ge(sem["r_late"], eng["on"] + eng["far"])
+    v.tensor_tensor(T.tb[:], T.rb[:], T.gb[:], AluOpType.mult).then_inc(sem["tbs"], 1)
+    v.wait_ge(sem["tbs"], 1)
+    v.tensor_tensor(T.yb[:], T.ta[:], T.tb[:], AluOpType.add).then_inc(sem["ys"], 1)
+    g.sync.wait_ge(sem["ys"], 1)
+    g.sync.dma_start(T.y[:], T.yb[:]).then_inc(sem["sty"], 16)
+    g.sync.wait_ge(sem["sty"], 16)
+    g.wait_ge(sem["sent"], sent[0])

@@ -5,9 +5,6 @@ NC = 128
 G = 4
 STEP = 1
 C = 0.019
-LEAST = 128
-XW = 512
-EW = 192
 
 SCRATCH = {
     "xb": ("sbuf", [128, 4 * NC], "bfloat16"),
@@ -17,44 +14,40 @@ SCRATCH = {
     "w1s": ("sbuf", [128, G * 128], "uint8"),
     "w2c": ("sbuf", [128, 128], "float8_e4m3fn_x4"),
     "w2s": ("sbuf", [128, 128], "uint8"),
-    "xc": ("sbuf", [128, XW], "float8_e4m3fn_x4"),
-    "xs": ("sbuf", [128, XW], "uint8"),
-    "hE": ("sbuf", [128, 4 * EW], "bfloat16"),
-    "hL": ("sbuf", [128, 4 * EW], "bfloat16"),
-    "hcE": ("sbuf", [128, EW], "float8_e4m3fn_x4"),
-    "hcL": ("sbuf", [128, EW], "float8_e4m3fn_x4"),
-    "hsE": ("sbuf", [128, EW], "uint8"),
-    "hsL": ("sbuf", [128, EW], "uint8"),
-    "pE": ("sbuf", [128, EW], "float32"),
-    "pL": ("sbuf", [128, EW], "float32"),
+    "v1c": ("sbuf", [128, G * 128], "float8_e4m3fn_x4"),
+    "v1s": ("sbuf", [128, G * 128], "uint8"),
+    "v2c": ("sbuf", [128, 128], "float8_e4m3fn_x4"),
+    "v2s": ("sbuf", [128, 128], "uint8"),
+    "xc": ("sbuf", [128, 2 * NC], "float8_e4m3fn_x4"),
+    "xs": ("sbuf", [128, 2 * NC], "uint8"),
+    "hA": ("sbuf", [128, 4 * NC], "bfloat16"),
+    "hB": ("sbuf", [128, 4 * NC], "bfloat16"),
+    "hcA": ("sbuf", [128, NC], "float8_e4m3fn_x4"),
+    "hsA": ("sbuf", [128, NC], "uint8"),
+    "hcB": ("sbuf", [128, NC], "float8_e4m3fn_x4"),
+    "hsB": ("sbuf", [128, NC], "uint8"),
+    "hcH": ("sbuf", [128, NC], "float8_e4m3fn_x4"),
+    "hsH": ("sbuf", [128, NC], "uint8"),
+    "hcO": ("sbuf", [128, NC], "float8_e4m3fn_x4"),
+    "hsO": ("sbuf", [128, NC], "uint8"),
+    "grow": ("sbuf", [1, 2 * NC], "bfloat16"),
+    "gf": ("sbuf", [128, NC], "bfloat16"),
+    "gn": ("sbuf", [128, NC], "bfloat16"),
+    "gall": ("sbuf", [128, 2 * NC], "bfloat16"),
+    "pA": ("sbuf", [128, NC], "float32"),
+    "pB": ("sbuf", [128, NC], "float32"),
+    "pO": ("sbuf", [128, NC], "float32"),
     "ra": ("sbuf", [128, NC], "float32"),
     "rb": ("sbuf", [128, NC], "float32"),
-    "grow": ("sbuf", [1, 2 * NC], "bfloat16"),
-    "gall": ("sbuf", [128, 2 * NC], "bfloat16"),
-    "gb": ("sbuf", [128, NC], "bfloat16"),
     "ta": ("sbuf", [128, NC], "float32"),
-    "tb": ("sbuf", [128, NC], "float32"),
+    "ht": ("sbuf", [128, NC], "float32"),
+    "ho": ("sbuf", [128, NC], "float32"),
     "yb": ("sbuf", [128, NC], "float32"),
     "ps": ("psum", [128, 512 * 8], "float32"),
 }
-SEMAPHORES = (["ldx", "ldw1a", "ldw1b", "ldw2", "ldg", "qx", "qw1a", "qw1b", "qw2", "gdone", "sent",
-               "x_near", "x_far", "x_on", "r_near", "r_late", "gbs", "tas", "tbs", "ys", "sty"]
-              + ["%s%s" % (n, b) for b in "EL" for n in ("z0", "z1", "z2", "z3", "as", "av", "hq", "p", "ev")])
-
-
-def run_of(cnt, j, e):
-    a = b = None
-    at = 0
-    for k in range(N):
-        w = cnt[j][k]
-        if w and (k == e or (k + STEP) % N == e):
-            if a is None:
-                a = at
-            elif b != at:
-                raise ValueError("not one run")
-            b = at + w
-        at += w
-    return (0, 0) if a is None else (a, b)
+SEMAPHORES = (["ldx", "ldw1a", "ldw1b", "ldw2", "ldg", "qx", "qw1a", "qw1b", "qw2", "gf", "gown", "sent",
+               "x_near", "gn", "ra", "rb", "v1", "v2", "pad", "hm", "tas", "ys", "sty", "evO", "evA", "evB"]
+              + ["%s%s" % (n, b) for b in "OABH" for n in ("z0", "z1", "z2", "z3", "as", "av", "hq", "p")])
 
 
 def peers_of(T, topo, e):
@@ -68,42 +61,32 @@ def peers_of(T, topo, e):
             out["on"] = j
         elif topo.die(c) == topo.die(d):
             out["near"] = j
-        else:
-            out["far"] = j
     return out
 
 
-def plan_of(T, topo, e):
-    cnt = T.tables["CNT"]
-    p = peers_of(T, topo, e)
-    wide = {}
-    for way in p:
-        a, b = run_of(cnt, p[way], e)
-        wide[way] = b - a
-    a0, b0 = run_of(cnt, e, e)
-    own = b0 - a0
-    if own and b0 != NC:
-        raise ValueError("own run must end the tile")
-    if own + wide["on"] + wide["far"] <= LEAST:
-        order, early, late = ("on", "far", "near"), ("near",), ("far", "on")
-    else:
-        if own:
-            raise ValueError("own run has no batch")
-        order, early, late = ("on", "near", "far"), ("on", "near"), ("far",)
-    at, lo = {}, NC
-    for way in order:
-        at[p[way]] = lo
-        lo += wide[way]
-    ends = {}
-    for name, ways in (("E", early), ("L", late)):
-        s = min(at[p[w]] for w in ways)
-        t = max(at[p[w]] + wide[w] for w in ways)
-        if name == "L":
-            s -= own
-        if t - s < LEAST:
-            s = t - LEAST
-        ends[name] = (s, t)
-    return {"peers": p, "at": at, "batch": ends, "ways": {"E": early, "L": late}}
+def pieces(cnt, j, row_of):
+    out, at = [], 0
+    for k in range(N):
+        w = cnt[j][k]
+        row = row_of(k, (k + STEP) % N)
+        if w and row is not None:
+            if out and out[-1][1] == at and out[-1][2] == row:
+                out[-1] = (out[-1][0], at + w, row)
+            else:
+                out.append((at, at + w, row))
+        at += w
+    return out
+
+
+def with_expert(cnt, j, e):
+    return pieces(cnt, j, lambda p, q: 0 if p == e else 1 if q == e else None)
+
+
+def span(segs):
+    for s, t in zip(segs, segs[1:]):
+        if s[1] != t[0]:
+            raise ValueError("not one run")
+    return segs[0][0], segs[-1][1]
 
 
 def rank_program(g, core, T, topo):
@@ -112,18 +95,30 @@ def rank_program(g, core, T, topo):
         return
     sem = T.sem
     cnt = T.tables["CNT"]
-    me = plan_of(T, topo, rank)
-    peers = me["peers"]
-    off_mask = topo.mask(core, T.cores[peers["near"]])
-    masks = {"near": off_mask, "far": topo.mask(core, T.cores[peers["far"]]),
-             "on": topo.mask(core, T.cores[peers["on"]]) & ~off_mask}
-    eng = {w: bin(masks[w]).count("1") for w in masks}
+    peers = peers_of(T, topo, rank)
+    on, near = peers["on"], peers["near"]
+    far = peers_of(T, topo, near)["on"]
+    off_mask = topo.mask(core, T.cores[near])
+    all_mask = topo.mask(core, T.cores[on])
+    in_mask = all_mask & ~off_mask
     sent = [0]
 
-    def send(way, out_ap, in_ap, remote_sem):
-        rid, pid = topo.addr(T.cores[peers[way]], core)
-        g.remote_dma(out_ap, in_ap, remote_sem, sem["sent"], pid, rid, masks[way])
-        sent[0] += eng[way]
+    def count(m):
+        return bin(m).count("1")
+
+    def send(to, mask, out_ap, in_ap, remote_sem):
+        rid, pid = topo.addr(T.cores[to], core)
+        g.remote_dma(out_ap, in_ap, sem[remote_sem], sem["sent"], pid, rid, mask)
+        sent[0] += count(mask)
+
+    sendA, sendB = with_expert(cnt, rank, near), with_expert(cnt, rank, far)
+    segA, segB = with_expert(cnt, near, rank), with_expert(cnt, near, on)
+    segH, segO = with_expert(cnt, rank, on), with_expert(cnt, rank, rank)
+    a0, b0 = span(sendA)
+    c0, c1 = span(segA)
+    for whole, part in (((a0, b0), span(sendB)), ((c0, c1), span(segB))):
+        if part[0] < whole[0] or part[1] > whole[1]:
+            raise ValueError("a token that leaves without needing the near expert")
 
     g.sync.dma_start(T.xb[:], T.x[:]).then_inc(sem["ldx"], 16)
     g.sync.dma_start(T.w1b[:, 0:1024], T.w1[:, 0:1024]).then_inc(sem["ldw1a"], 16)
@@ -142,99 +137,158 @@ def rank_program(g, core, T, topo):
     v.quantize_mx(T.w2c[:], T.w2s[:], T.w2b[:]).then_inc(sem["qw2"], 1)
 
     g.wait_ge(sem["qx"], 1)
-    for way in ("near", "far", "on"):
-        e = peers[way]
-        a, b = run_of(cnt, rank, e)
-        d = plan_of(T, topo, e)["at"][rank]
-        send(way, T.xc[:, d:d + b - a].bitcast(dt.uint8), T.xc[:, a:b].bitcast(dt.uint8), sem["x_" + way])
-        send(way, T.xs[:, d:d + b - a], T.xs[:, a:b], sem["x_" + way])
-
+    n = b0 - a0
+    send(near, off_mask, T.xc[:, NC:NC + n].bitcast(dt.uint8), T.xc[:, a0:b0].bitcast(dt.uint8), "x_near")
+    send(near, off_mask, T.xs[:, NC:NC + n], T.xs[:, a0:b0], "x_near")
+    g.wait_ge(sem["qw1a"], 1)
+    send(on, in_mask, T.v1c[:, 0:256].bitcast(dt.uint8), T.w1c[:, 0:256].bitcast(dt.uint8), "v1")
+    g.wait_ge(sem["qw1b"], 1)
+    send(on, off_mask, T.v1c[:, 256:512].bitcast(dt.uint8), T.w1c[:, 256:512].bitcast(dt.uint8), "v1")
+    send(on, in_mask, T.v1s[:], T.w1s[:], "v1")
+    all_v1 = count(in_mask) + count(off_mask) + count(in_mask)
+    g.wait_ge(sem["qw2"], 1)
+    send(on, all_mask, T.v2c[:].bitcast(dt.uint8), T.w2c[:].bitcast(dt.uint8), "v2")
+    send(on, all_mask, T.v2s[:], T.w2s[:], "v2")
+    all_v2 = 2 * count(all_mask)
     g.wait_ge(sem["ldg"], 16)
-    g.partition_broadcast(T.gall[:], T.grow[:], 128).then_inc(sem["gdone"], 1)
+    for a, z, row in sendB:
+        g.partition_broadcast(T.gf[:, a:z], T.grow[:, NC * row + a:NC * row + z], 128).then_inc(sem["gf"], 1)
+    a, z = span(sendB)
+    g.wait_ge(sem["gf"], len(sendB))
+    send(near, off_mask, T.gn[:, a:z], T.gf[:, a:z], "gn")
+    g.partition_broadcast(T.gall[:], T.grow[:], 128).then_inc(sem["gown"], 1)
+    for land, share, done, seg in ((T.ra, T.pA, "A", segA), (T.rb, T.pB, "B", segB)):
+        a, z = span(seg)
+        g.wait_ge(sem["ev" + done], 1)
+        send(near, off_mask, land[:, a:z], share[:, a:z], "r" + done.lower())
 
     t = g.tensor
-    banks = {"E": (0, 1, 2, 3, 4), "L": (5, 6, 7, 0, 1)}
+    s = g.scalar
+    banks = {"O": (4, 5, 6, 7, 4), "A": (0, 1, 2, 3, 0), "B": (4, 5, 6, 7, 4), "H": (1, 2, 3, 5, 6)}
+    mine = (T.w1c, T.w1s, T.w2c, T.w2s)
+    other = (T.v1c, T.v1s, T.v2c, T.v2s)
+    weights = {"O": mine, "A": mine, "B": other, "H": other}
+    tiles = {"O": T.hA, "A": T.hA, "B": T.hB, "H": T.hA}
+    first = {"O": 0, "A": c1 - c0, "B": span(segB)[1] - c0, "H": 0}
+    base = {"O": 0, "H": 0, "A": NC - c0 - first["A"], "B": NC - c0 - first["B"]}
 
-    def bank(b, k, lo, hi):
+    def bank(b, k, lo=0, hi=NC):
         return T.ps[:, 512 * banks[b][k] + lo:512 * banks[b][k] + hi]
 
-    def back(b, way):
-        a, z = run_of(cnt, peers[way], rank)
-        s = me["at"][peers[way]] - me["batch"][b][0]
-        return s, s + z - a, a, z
-
-    for b in "EL":
-        ways = me["ways"][b]
-        lo, hi = me["batch"][b]
-        n = hi - lo
-        h, hc, hs, p = T["h" + b], T["hc" + b], T["hs" + b], T["p" + b]
-        t.wait_ge(sem["qw1a" if b == "E" else "qx"], 1)
-        for way in ways:
-            t.wait_ge(sem["x_" + way], 2 * eng[way])
+    def first_products(b):
+        w1c, w1s = weights[b][:2]
         for k in range(G):
-            if b == "E" and k == 2:
-                t.wait_ge(sem["qw1b"], 1)
             w = slice(128 * k, 128 * k + 128)
-            t.matmul_mx(bank(b, k, 0, n), T.w1c[:, w], T.w1s[:, w], T.xc[:, lo:hi], T.xs[:, lo:hi],
-                        True, True).then_inc(sem["z%d%s" % (k, b)], 1)
+            t.matmul_mx(bank(b, k), w1c[:, w], w1s[:, w], T.xc[:, first[b]:first[b] + NC],
+                        T.xs[:, first[b]:first[b] + NC], True, True).then_inc(sem["z%d%s" % (k, b)], 1)
+
+    def second_product(b):
+        w2c, w2s = weights[b][2:]
+        t.wait_ge(sem["hq" + b], 1)
+        t.matmul_mx(bank(b, 4), w2c[:], w2s[:], T["hc" + b][:], T["hs" + b][:], True, True).then_inc(sem["p" + b], 1)
+
+    def tile_scalar(b, lo=0, hi=NC):
         for k in (0, 2):
-            g.scalar.wait_ge(sem["z%d%s" % (k, b)], 1)
-            g.scalar.activation(h[:, k:4 * n:4], bank(b, k, 0, n), ActivationFunctionType.Relu,
-                                scale=C).then_inc(sem["as" + b], 1)
+            s.wait_ge(sem["z%d%s" % (k, b)], 1)
+            s.activation(tiles[b][:, 4 * lo + k:4 * hi:4], bank(b, k, lo, hi), ActivationFunctionType.Relu,
+                         scale=C).then_inc(sem["as" + b], 1)
+
+    def tile_vector(b, lo=0, hi=NC):
         for k in (1, 3):
             v.wait_ge(sem["z%d%s" % (k, b)], 1)
-            v.tensor_scalar(h[:, k:4 * n:4], bank(b, k, 0, n), 0.0, C, AluOpType.max,
+            v.tensor_scalar(tiles[b][:, 4 * lo + k:4 * hi:4], bank(b, k, lo, hi), 0.0, C, AluOpType.max,
                             AluOpType.mult).then_inc(sem["av" + b], 1)
+
+    def pack(b):
         v.wait_ge(sem["as" + b], 2)
         v.wait_ge(sem["av" + b], 2)
-        v.quantize_mx(hc[:, 0:n], hs[:, 0:n], h[:, 0:4 * n]).then_inc(sem["hq" + b], 1)
-        if b == "E":
-            t.wait_ge(sem["qw2"], 1)
-        t.wait_ge(sem["hq" + b], 1)
-        t.matmul_mx(bank(b, 4, 0, n), T.w2c[:], T.w2s[:], hc[:, 0:n], hs[:, 0:n], True, True).then_inc(sem["p" + b], 1)
-        pieces = [back(b, w) for w in ways]
-        s0, s1 = min(q[0] for q in pieces), max(q[1] for q in pieces)
-        if b == "E":
-            g.scalar.wait_ge(sem["p" + b], 1)
-            g.scalar.activation(p[:, s0:s1], bank(b, 4, s0, s1), ActivationFunctionType.Copy).then_inc(sem["ev" + b], 1)
-        else:
-            v.wait_ge(sem["p" + b], 1)
-            v.tensor_copy(p[:, s0:s1], bank(b, 4, s0, s1)).then_inc(sem["ev" + b], 1)
-        g.wait_ge(sem["ev" + b], 1)
-        for way in sorted(ways, key=lambda w: w == "on"):
-            s, z, a, c = back(b, way)
-            send(way, T["ra" if way == "near" else "rb"][:, a:c], p[:, s:z], sem["r_near" if way == "near" else "r_late"])
+        v.quantize_mx(T["hc" + b][:], T["hs" + b][:], tiles[b][:]).then_inc(sem["hq" + b], 1)
 
-    segs, at = [], 0
-    for k in range(N):
-        w = cnt[rank][k]
-        if w:
-            pair = (k, (k + STEP) % N)
-            mine = peers["near"] if peers["near"] in pair else rank
-            if mine not in pair:
-                raise ValueError("no near or own expert")
-            segs.append((at, at + w, 0 if pair[0] == mine else 1, mine == rank))
-        at += w
-    v.wait_ge(sem["gdone"], 1)
-    for a, z, row, _own in segs:
-        o = NC * (1 - row)
-        v.tensor_copy(T.gb[:, a:z], T.gall[:, o + a:o + z]).then_inc(sem["gbs"], 1)
-    for own_turn in (True, False):
-        if not own_turn:
-            v.wait_ge(sem["r_near"], eng["near"])
-        for a, z, row, is_own in segs:
-            if is_own == own_turn:
-                lo = me["batch"]["L"][0]
-                src = bank("L", 4, a - lo, z - lo) if is_own else T.ra[:, a:z]
-                v.tensor_tensor(T.ta[:, a:z], src, T.gall[:, NC * row + a:NC * row + z],
-                                AluOpType.mult).then_inc(sem["tas"], 1)
-    v.wait_ge(sem["gbs"], len(segs))
-    v.wait_ge(sem["tas"], len(segs))
-    v.wait_ge(sem["r_late"], eng["on"] + eng["far"])
-    v.tensor_tensor(T.tb[:], T.rb[:], T.gb[:], AluOpType.mult).then_inc(sem["tbs"], 1)
-    v.wait_ge(sem["tbs"], 1)
-    v.tensor_tensor(T.yb[:], T.ta[:], T.tb[:], AluOpType.add).then_inc(sem["ys"], 1)
-    g.sync.wait_ge(sem["ys"], 1)
+    wantB = [x + base["B"] for x in span(segB)]
+    wantH = span(segH)
+
+    t.wait_ge(sem["qx"], 1)
+    t.wait_ge(sem["qw1a"], 1)
+    t.wait_ge(sem["qw1b"], 1)
+    if segO:
+        first_products("O")
+        t.wait_ge(sem["qw2"], 1)
+        second_product("O")
+    t.wait_ge(sem["x_near"], 2 * count(off_mask))
+    first_products("A")
+    t.wait_ge(sem["v1"], all_v1)
+    if segO:
+        t.wait_ge(sem["evO"], 1)
+    first_products("B")
+    if not segO:
+        t.wait_ge(sem["qw2"], 1)
+    second_product("A")
+    t.wait_ge(sem["v2"], all_v2)
+    second_product("B")
+    first_products("H")
+    second_product("H")
+
+    if segO:
+        tile_scalar("O")
+        a, z = span(segO)
+        s.wait_ge(sem["pO"], 1)
+        s.activation(T.pO[:, a:z], bank("O", 4, a, z), ActivationFunctionType.Copy).then_inc(sem["evO"], 1)
+        s.wait_ge(sem["hqO"], 1)
+    tile_scalar("A")
+    s.wait_ge(sem["pad"], 1)
+    tile_scalar("B", *wantB)
+    a, z = span(segA)
+    s.wait_ge(sem["pA"], 1)
+    s.activation(T.pA[:, a:z], bank("A", 4, a + base["A"], z + base["A"]),
+                 ActivationFunctionType.Copy).then_inc(sem["evA"], 1)
+    tile_scalar("H", *wantH)
+
+    if wantB[1] != NC or not wantB[0]:
+        raise ValueError("B's wanted columns end its tile")
+    v.memset(T.hB[:, 0:4 * wantB[0]], 0.0).then_inc(sem["pad"], 1)
+    if segO:
+        tile_vector("O")
+        pack("O")
+        v.wait_ge(sem["hqO"], 1)
+    tile_vector("A")
+    pack("A")
+    v.wait_ge(sem["pad"], 1)
+    tile_vector("B", *wantB)
+    pack("B")
+    a, z = span(segB)
+    v.wait_ge(sem["gn"], count(off_mask))
+    v.wait_ge(sem["pB"], 1)
+    v.tensor_tensor(T.pB[:, a:z], bank("B", 4, a + base["B"], z + base["B"]), T.gn[:, a:z],
+                    AluOpType.mult).then_inc(sem["evB"], 1)
+    v.wait_ge(sem["hqA"], 1)
+    tile_vector("H", *wantH)
+    pack("H")
+
+    v.wait_ge(sem["gown"], 1)
+
+    def gated(out, src, segs, done):
+        for a, z, row in segs:
+            v.tensor_tensor(out[:, a:z], src(a, z), T.gall[:, NC * row + a:NC * row + z],
+                            AluOpType.mult).then_inc(sem[done], 1)
+
+    def summed(a, z, p, q):
+        v.tensor_tensor(T.yb[:, a:z], p[:, a:z], q[:, a:z], AluOpType.add).then_inc(sem["ys"], 1)
+
+    both = pieces(cnt, rank, lambda p, q: 0 if rank in (p, q) else None)
+    half = pieces(cnt, rank, lambda p, q: 0 if on in (p, q) and rank not in (p, q) else None)
+    gated(T.ho, lambda a, z: T.pO[:, a:z], segO, "hm")
+    v.wait_ge(sem["pH"], 1)
+    gated(T.ht, lambda a, z: bank("H", 4, a, z), segH, "hm")
+    v.wait_ge(sem["ra"], count(off_mask))
+    gated(T.ta, lambda a, z: T.ra[:, a:z], sendA, "tas")
+    v.wait_ge(sem["hm"], len(segO) + len(segH))
+    for a, z, _row in both:
+        summed(a, z, T.ht, T.ho)
+    v.wait_ge(sem["tas"], len(sendA))
+    summed(*span(half), T.ta, T.ht)
+    v.wait_ge(sem["rb"], count(off_mask))
+    summed(*span(sendB), T.ta, T.rb)
+    g.sync.wait_ge(sem["ys"], len(both) + 2)
     g.sync.dma_start(T.y[:], T.yb[:]).then_inc(sem["sty"], 16)
     g.sync.wait_ge(sem["sty"], 16)
     g.wait_ge(sem["sent"], sent[0])

@@ -5,6 +5,7 @@ NC = 128
 G = 4
 STEP = 1
 C = 0.019
+HEAD = 2
 
 SCRATCH = {
     "xb": ("sbuf", [128, 4 * NC], "bfloat16"),
@@ -30,10 +31,12 @@ SCRATCH = {
     "hsH": ("sbuf", [128, NC], "uint8"),
     "hcO": ("sbuf", [128, NC], "float8_e4m3fn_x4"),
     "hsO": ("sbuf", [128, NC], "uint8"),
+    "gd": ("dram", [128, 2], "bfloat16"),
+    "ge": ("dram", [128, 2], "bfloat16"),
     "grow": ("sbuf", [1, 2 * NC], "bfloat16"),
-    "gf": ("sbuf", [128, NC], "bfloat16"),
-    "gn": ("sbuf", [128, NC], "bfloat16"),
+    "grown": ("sbuf", [1, 2 * NC], "bfloat16"),
     "gall": ("sbuf", [128, 2 * NC], "bfloat16"),
+    "galn": ("sbuf", [128, NC], "bfloat16"),
     "pA": ("sbuf", [128, NC], "float32"),
     "pB": ("sbuf", [128, NC], "float32"),
     "pO": ("sbuf", [128, NC], "float32"),
@@ -45,8 +48,8 @@ SCRATCH = {
     "yb": ("sbuf", [128, NC], "float32"),
     "ps": ("psum", [128, 512 * 8], "float32"),
 }
-SEMAPHORES = (["ldx", "ldw1a", "ldw1b", "ldw2", "ldg", "qx", "qw1a", "qw1b", "qw2", "gf", "gown", "sent",
-               "x_near", "gn", "ra", "rb", "v1", "v2", "pad", "hm", "tas", "ys", "sty", "evO", "evA", "evB"]
+SEMAPHORES = (["ldx", "ldw1a", "ldw1b", "ldw2", "ldg", "ldgd", "ldgn", "qx", "qw1a", "qw1b", "qw2", "gown", "gnear", "sent",
+               "g_in", "x_in", "ra", "rb", "v1a", "v1b", "v2", "pad", "hm", "tas", "ys", "sty", "evO", "evA", "evB"]
               + ["%s%s" % (n, b) for b in "OABH" for n in ("z0", "z1", "z2", "z3", "as", "av", "hq", "p")])
 
 
@@ -120,11 +123,14 @@ def rank_program(g, core, T, topo):
         if part[0] < whole[0] or part[1] > whole[1]:
             raise ValueError("a token that leaves without needing the near expert")
 
+    g.sync.dma_start(T.gd[:], T.gt[:]).then_inc(sem["ldgd"], 16)
     g.sync.dma_start(T.xb[:], T.x[:]).then_inc(sem["ldx"], 16)
     g.sync.dma_start(T.w1b[:, 0:1024], T.w1[:, 0:1024]).then_inc(sem["ldw1a"], 16)
     g.sync.dma_start(T.w1b[:, 1024:2048], T.w1[:, 1024:2048]).then_inc(sem["ldw1b"], 16)
     g.sync.dma_start(T.w2b[:], T.w2[:]).then_inc(sem["ldw2"], 16)
     g.scalar.dma_start(T.grow[:], T.gt[:]).then_inc(sem["ldg"], 16)
+    g.sync.wait_ge(sem["g_in"], count(off_mask))
+    g.sync.dma_start(T.grown[:], T.ge[:]).then_inc(sem["ldgn"], 16)
 
     v = g.vector
     v.wait_ge(sem["ldx"], 16)
@@ -136,31 +142,31 @@ def rank_program(g, core, T, topo):
     v.wait_ge(sem["ldw2"], 16)
     v.quantize_mx(T.w2c[:], T.w2s[:], T.w2b[:]).then_inc(sem["qw2"], 1)
 
+    g.wait_ge(sem["ldgd"], 16)
+    send(near, off_mask, T.ge[:], T.gd[:], "g_in")
     g.wait_ge(sem["qx"], 1)
     n = b0 - a0
-    send(near, off_mask, T.xc[:, NC:NC + n].bitcast(dt.uint8), T.xc[:, a0:b0].bitcast(dt.uint8), "x_near")
-    send(near, off_mask, T.xs[:, NC:NC + n], T.xs[:, a0:b0], "x_near")
+    send(near, off_mask, T.xc[:, NC:NC + n].bitcast(dt.uint8), T.xc[:, a0:b0].bitcast(dt.uint8), "x_in")
+    send(near, off_mask, T.xs[:, NC:NC + n], T.xs[:, a0:b0], "x_in")
     g.wait_ge(sem["qw1a"], 1)
-    send(on, in_mask, T.v1c[:, 0:256].bitcast(dt.uint8), T.w1c[:, 0:256].bitcast(dt.uint8), "v1")
+    send(on, all_mask, T.v1c[:, 0:256].bitcast(dt.uint8), T.w1c[:, 0:256].bitcast(dt.uint8), "v1a")
     g.wait_ge(sem["qw1b"], 1)
-    send(on, off_mask, T.v1c[:, 256:512].bitcast(dt.uint8), T.w1c[:, 256:512].bitcast(dt.uint8), "v1")
-    send(on, in_mask, T.v1s[:], T.w1s[:], "v1")
-    all_v1 = count(in_mask) + count(off_mask) + count(in_mask)
+    send(on, in_mask, T.v1s[:], T.w1s[:], "v1a")
+    send(on, all_mask, T.v1c[:, 256:512].bitcast(dt.uint8), T.w1c[:, 256:512].bitcast(dt.uint8), "v1b")
     g.wait_ge(sem["qw2"], 1)
     send(on, all_mask, T.v2c[:].bitcast(dt.uint8), T.w2c[:].bitcast(dt.uint8), "v2")
     send(on, all_mask, T.v2s[:], T.w2s[:], "v2")
-    all_v2 = 2 * count(all_mask)
+    ends = [NC * row + x for a, z, row in sendA + segH + segO for x in (a, z)]
+    lo, hi = min(ends), max(ends)
     g.wait_ge(sem["ldg"], 16)
-    for a, z, row in sendB:
-        g.partition_broadcast(T.gf[:, a:z], T.grow[:, NC * row + a:NC * row + z], 128).then_inc(sem["gf"], 1)
-    a, z = span(sendB)
-    g.wait_ge(sem["gf"], len(sendB))
-    send(near, off_mask, T.gn[:, a:z], T.gf[:, a:z], "gn")
-    g.partition_broadcast(T.gall[:], T.grow[:], 128).then_inc(sem["gown"], 1)
-    for land, share, done, seg in ((T.ra, T.pA, "A", segA), (T.rb, T.pB, "B", segB)):
+    g.partition_broadcast(T.gall[:, lo:hi], T.grow[:, lo:hi], 128).then_inc(sem["gown"], 1)
+    g.wait_ge(sem["ldgn"], 16)
+    for a, z, row in segB:
+        g.partition_broadcast(T.galn[:, a:z], T.grown[:, NC * row + a:NC * row + z], 128).then_inc(sem["gnear"], 1)
+    for land, share, b, seg in ((T.ra, T.pA, "A", segA), (T.rb, T.pB, "B", segB)):
         a, z = span(seg)
-        g.wait_ge(sem["ev" + done], 1)
-        send(near, off_mask, land[:, a:z], share[:, a:z], "r" + done.lower())
+        g.wait_ge(sem["ev" + b], 1)
+        send(near, off_mask, land[:, a:z], share[:, a:z], "r" + b.lower())
 
     t = g.tensor
     s = g.scalar
@@ -175,9 +181,9 @@ def rank_program(g, core, T, topo):
     def bank(b, k, lo=0, hi=NC):
         return T.ps[:, 512 * banks[b][k] + lo:512 * banks[b][k] + hi]
 
-    def first_products(b):
+    def first_products(b, ks=range(G)):
         w1c, w1s = weights[b][:2]
-        for k in range(G):
+        for k in ks:
             w = slice(128 * k, 128 * k + 128)
             t.matmul_mx(bank(b, k), w1c[:, w], w1s[:, w], T.xc[:, first[b]:first[b] + NC],
                         T.xs[:, first[b]:first[b] + NC], True, True).then_inc(sem["z%d%s" % (k, b)], 1)
@@ -214,18 +220,21 @@ def rank_program(g, core, T, topo):
         first_products("O")
         t.wait_ge(sem["qw2"], 1)
         second_product("O")
-    t.wait_ge(sem["x_near"], 2 * count(off_mask))
+    t.wait_ge(sem["x_in"], 2 * count(off_mask))
     first_products("A")
-    t.wait_ge(sem["v1"], all_v1)
+    t.wait_ge(sem["v1a"], count(all_mask) + count(in_mask))
     if segO:
         t.wait_ge(sem["evO"], 1)
-    first_products("B")
+    first_products("B", (0, 1))
+    t.wait_ge(sem["v1b"], count(all_mask))
+    first_products("B", (2, 3))
     if not segO:
         t.wait_ge(sem["qw2"], 1)
     second_product("A")
-    t.wait_ge(sem["v2"], all_v2)
+    first_products("H", range(HEAD))
+    t.wait_ge(sem["v2"], 2 * count(all_mask))
     second_product("B")
-    first_products("H")
+    first_products("H", range(HEAD, G))
     second_product("H")
 
     if segO:
@@ -255,10 +264,10 @@ def rank_program(g, core, T, topo):
     v.wait_ge(sem["pad"], 1)
     tile_vector("B", *wantB)
     pack("B")
-    a, z = span(segB)
-    v.wait_ge(sem["gn"], count(off_mask))
+    v.wait_ge(sem["gnear"], len(segB))
     v.wait_ge(sem["pB"], 1)
-    v.tensor_tensor(T.pB[:, a:z], bank("B", 4, a + base["B"], z + base["B"]), T.gn[:, a:z],
+    a, z = span(segB)
+    v.tensor_tensor(T.pB[:, a:z], bank("B", 4, a + base["B"], z + base["B"]), T.galn[:, a:z],
                     AluOpType.mult).then_inc(sem["evB"], 1)
     v.wait_ge(sem["hqA"], 1)
     tile_vector("H", *wantH)

from concourse.mybir import dt, AluOpType, ActivationFunctionType

N = 4
NC = 128
G = 4
STEP = 1
C = 0.019
HEAD = 2

SCRATCH = {
    "xb": ("sbuf", [128, 4 * NC], "bfloat16"),
    "w1b": ("sbuf", [128, G * 512], "bfloat16"),
    "w2b": ("sbuf", [128, 512], "bfloat16"),
    "w1c": ("sbuf", [128, G * 128], "float8_e4m3fn_x4"),
    "w1s": ("sbuf", [128, G * 128], "uint8"),
    "w2c": ("sbuf", [128, 128], "float8_e4m3fn_x4"),
    "w2s": ("sbuf", [128, 128], "uint8"),
    "v1c": ("sbuf", [128, G * 128], "float8_e4m3fn_x4"),
    "v1s": ("sbuf", [128, G * 128], "uint8"),
    "v2c": ("sbuf", [128, 128], "float8_e4m3fn_x4"),
    "v2s": ("sbuf", [128, 128], "uint8"),
    "xc": ("sbuf", [128, 2 * NC], "float8_e4m3fn_x4"),
    "xs": ("sbuf", [128, 2 * NC], "uint8"),
    "hA": ("sbuf", [128, 4 * NC], "bfloat16"),
    "hB": ("sbuf", [128, 4 * NC], "bfloat16"),
    "hcA": ("sbuf", [128, NC], "float8_e4m3fn_x4"),
    "hsA": ("sbuf", [128, NC], "uint8"),
    "hcB": ("sbuf", [128, NC], "float8_e4m3fn_x4"),
    "hsB": ("sbuf", [128, NC], "uint8"),
    "hcH": ("sbuf", [128, NC], "float8_e4m3fn_x4"),
    "hsH": ("sbuf", [128, NC], "uint8"),
    "hcO": ("sbuf", [128, NC], "float8_e4m3fn_x4"),
    "hsO": ("sbuf", [128, NC], "uint8"),
    "gd": ("dram", [128, 2], "bfloat16"),
    "ge": ("dram", [128, 2], "bfloat16"),
    "grow": ("sbuf", [1, 2 * NC], "bfloat16"),
    "grown": ("sbuf", [1, 2 * NC], "bfloat16"),
    "gall": ("sbuf", [128, 2 * NC], "bfloat16"),
    "galn": ("sbuf", [128, NC], "bfloat16"),
    "pA": ("sbuf", [128, NC], "float32"),
    "pB": ("sbuf", [128, NC], "float32"),
    "pO": ("sbuf", [128, NC], "float32"),
    "ra": ("sbuf", [128, NC], "float32"),
    "rb": ("sbuf", [128, NC], "float32"),
    "ta": ("sbuf", [128, NC], "float32"),
    "ht": ("sbuf", [128, NC], "float32"),
    "ho": ("sbuf", [128, NC], "float32"),
    "yb": ("sbuf", [128, NC], "float32"),
    "ps": ("psum", [128, 512 * 8], "float32"),
}
SEMAPHORES = (["ldx", "ldw1a", "ldw1b", "ldw2", "ldg", "ldgd", "ldgn", "qx", "qw1a", "qw1b", "qw2", "gown", "gnear", "sent",
               "g_in", "x_in", "ra", "rb", "v1a", "v1b", "v2", "pad", "hm", "tas", "ys", "sty", "evO", "evA", "evB"]
              + ["%s%s" % (n, b) for b in "OABH" for n in ("z0", "z1", "z2", "z3", "as", "av", "hq", "p")])


def peers_of(T, topo, e):
    c = T.cores[e]
    out = {}
    for j in range(N):
        d = T.cores[j]
        if j == e:
            continue
        if (topo.host(c), topo.chip(c)) == (topo.host(d), topo.chip(d)):
            out["on"] = j
        elif topo.die(c) == topo.die(d):
            out["near"] = j
    return out


def pieces(cnt, j, row_of):
    out, at = [], 0
    for k in range(N):
        w = cnt[j][k]
        row = row_of(k, (k + STEP) % N)
        if w and row is not None:
            if out and out[-1][1] == at and out[-1][2] == row:
                out[-1] = (out[-1][0], at + w, row)
            else:
                out.append((at, at + w, row))
        at += w
    return out


def with_expert(cnt, j, e):
    return pieces(cnt, j, lambda p, q: 0 if p == e else 1 if q == e else None)


def span(segs):
    for s, t in zip(segs, segs[1:]):
        if s[1] != t[0]:
            raise ValueError("not one run")
    return segs[0][0], segs[-1][1]


def rank_program(g, core, T, topo):
    rank = T.rank_of(core)
    if rank is None:
        return
    sem = T.sem
    cnt = T.tables["CNT"]
    peers = peers_of(T, topo, rank)
    on, near = peers["on"], peers["near"]
    far = peers_of(T, topo, near)["on"]
    off_mask = topo.mask(core, T.cores[near])
    all_mask = topo.mask(core, T.cores[on])
    in_mask = all_mask & ~off_mask
    sent = [0]

    def count(m):
        return bin(m).count("1")

    def send(to, mask, out_ap, in_ap, remote_sem):
        rid, pid = topo.addr(T.cores[to], core)
        g.remote_dma(out_ap, in_ap, sem[remote_sem], sem["sent"], pid, rid, mask)
        sent[0] += count(mask)

    sendA, sendB = with_expert(cnt, rank, near), with_expert(cnt, rank, far)
    segA, segB = with_expert(cnt, near, rank), with_expert(cnt, near, on)
    segH, segO = with_expert(cnt, rank, on), with_expert(cnt, rank, rank)
    a0, b0 = span(sendA)
    c0, c1 = span(segA)
    for whole, part in (((a0, b0), span(sendB)), ((c0, c1), span(segB))):
        if part[0] < whole[0] or part[1] > whole[1]:
            raise ValueError("a token that leaves without needing the near expert")

    g.sync.dma_start(T.gd[:], T.gt[:]).then_inc(sem["ldgd"], 16)
    g.sync.dma_start(T.xb[:], T.x[:]).then_inc(sem["ldx"], 16)
    g.sync.dma_start(T.w1b[:, 0:1024], T.w1[:, 0:1024]).then_inc(sem["ldw1a"], 16)
    g.sync.dma_start(T.w1b[:, 1024:2048], T.w1[:, 1024:2048]).then_inc(sem["ldw1b"], 16)
    g.sync.dma_start(T.w2b[:], T.w2[:]).then_inc(sem["ldw2"], 16)
    g.scalar.dma_start(T.grow[:], T.gt[:]).then_inc(sem["ldg"], 16)
    g.sync.wait_ge(sem["g_in"], count(off_mask))
    g.sync.dma_start(T.grown[:], T.ge[:]).then_inc(sem["ldgn"], 16)

    v = g.vector
    v.wait_ge(sem["ldx"], 16)
    v.quantize_mx(T.xc[:, 0:NC], T.xs[:, 0:NC], T.xb[:]).then_inc(sem["qx"], 1)
    v.wait_ge(sem["ldw1a"], 16)
    v.quantize_mx(T.w1c[:, 0:256], T.w1s[:, 0:256], T.w1b[:, 0:1024]).then_inc(sem["qw1a"], 1)
    v.wait_ge(sem["ldw1b"], 16)
    v.quantize_mx(T.w1c[:, 256:512], T.w1s[:, 256:512], T.w1b[:, 1024:2048]).then_inc(sem["qw1b"], 1)
    v.wait_ge(sem["ldw2"], 16)
    v.quantize_mx(T.w2c[:], T.w2s[:], T.w2b[:]).then_inc(sem["qw2"], 1)

    g.wait_ge(sem["ldgd"], 16)
    send(near, off_mask, T.ge[:], T.gd[:], "g_in")
    g.wait_ge(sem["qx"], 1)
    n = b0 - a0
    send(near, off_mask, T.xc[:, NC:NC + n].bitcast(dt.uint8), T.xc[:, a0:b0].bitcast(dt.uint8), "x_in")
    send(near, off_mask, T.xs[:, NC:NC + n], T.xs[:, a0:b0], "x_in")
    g.wait_ge(sem["qw1a"], 1)
    send(on, all_mask, T.v1c[:, 0:256].bitcast(dt.uint8), T.w1c[:, 0:256].bitcast(dt.uint8), "v1a")
    g.wait_ge(sem["qw1b"], 1)
    send(on, in_mask, T.v1s[:], T.w1s[:], "v1a")
    send(on, all_mask, T.v1c[:, 256:512].bitcast(dt.uint8), T.w1c[:, 256:512].bitcast(dt.uint8), "v1b")
    g.wait_ge(sem["qw2"], 1)
    send(on, all_mask, T.v2c[:].bitcast(dt.uint8), T.w2c[:].bitcast(dt.uint8), "v2")
    send(on, all_mask, T.v2s[:], T.w2s[:], "v2")
    ends = [NC * row + x for a, z, row in sendA + segH + segO for x in (a, z)]
    lo, hi = min(ends), max(ends)
    g.wait_ge(sem["ldg"], 16)
    g.partition_broadcast(T.gall[:, lo:hi], T.grow[:, lo:hi], 128).then_inc(sem["gown"], 1)
    g.wait_ge(sem["ldgn"], 16)
    for a, z, row in segB:
        g.partition_broadcast(T.galn[:, a:z], T.grown[:, NC * row + a:NC * row + z], 128).then_inc(sem["gnear"], 1)
    for land, share, b, seg in ((T.ra, T.pA, "A", segA), (T.rb, T.pB, "B", segB)):
        a, z = span(seg)
        g.wait_ge(sem["ev" + b], 1)
        send(near, off_mask, land[:, a:z], share[:, a:z], "r" + b.lower())

    t = g.tensor
    s = g.scalar
    banks = {"O": (4, 5, 6, 7, 4), "A": (0, 1, 2, 3, 0), "B": (4, 5, 6, 7, 4), "H": (1, 2, 3, 5, 6)}
    mine = (T.w1c, T.w1s, T.w2c, T.w2s)
    other = (T.v1c, T.v1s, T.v2c, T.v2s)
    weights = {"O": mine, "A": mine, "B": other, "H": other}
    tiles = {"O": T.hA, "A": T.hA, "B": T.hB, "H": T.hA}
    first = {"O": 0, "A": c1 - c0, "B": span(segB)[1] - c0, "H": 0}
    base = {"O": 0, "H": 0, "A": NC - c0 - first["A"], "B": NC - c0 - first["B"]}

    def bank(b, k, lo=0, hi=NC):
        return T.ps[:, 512 * banks[b][k] + lo:512 * banks[b][k] + hi]

    def first_products(b, ks=range(G)):
        w1c, w1s = weights[b][:2]
        for k in ks:
            w = slice(128 * k, 128 * k + 128)
            t.matmul_mx(bank(b, k), w1c[:, w], w1s[:, w], T.xc[:, first[b]:first[b] + NC],
                        T.xs[:, first[b]:first[b] + NC], True, True).then_inc(sem["z%d%s" % (k, b)], 1)

    def second_product(b):
        w2c, w2s = weights[b][2:]
        t.wait_ge(sem["hq" + b], 1)
        t.matmul_mx(bank(b, 4), w2c[:], w2s[:], T["hc" + b][:], T["hs" + b][:], True, True).then_inc(sem["p" + b], 1)

    def tile_scalar(b, lo=0, hi=NC):
        for k in (0, 2):
            s.wait_ge(sem["z%d%s" % (k, b)], 1)
            s.activation(tiles[b][:, 4 * lo + k:4 * hi:4], bank(b, k, lo, hi), ActivationFunctionType.Relu,
                         scale=C).then_inc(sem["as" + b], 1)

    def tile_vector(b, lo=0, hi=NC):
        for k in (1, 3):
            v.wait_ge(sem["z%d%s" % (k, b)], 1)
            v.tensor_scalar(tiles[b][:, 4 * lo + k:4 * hi:4], bank(b, k, lo, hi), 0.0, C, AluOpType.max,
                            AluOpType.mult).then_inc(sem["av" + b], 1)

    def pack(b):
        v.wait_ge(sem["as" + b], 2)
        v.wait_ge(sem["av" + b], 2)
        v.quantize_mx(T["hc" + b][:], T["hs" + b][:], tiles[b][:]).then_inc(sem["hq" + b], 1)

    wantB = [x + base["B"] for x in span(segB)]
    wantH = span(segH)

    t.wait_ge(sem["qx"], 1)
    t.wait_ge(sem["qw1a"], 1)
    t.wait_ge(sem["qw1b"], 1)
    if segO:
        first_products("O")
        t.wait_ge(sem["qw2"], 1)
        second_product("O")
    t.wait_ge(sem["x_in"], 2 * count(off_mask))
    first_products("A")
    t.wait_ge(sem["v1a"], count(all_mask) + count(in_mask))
    if segO:
        t.wait_ge(sem["evO"], 1)
    first_products("B", (0, 1))
    t.wait_ge(sem["v1b"], count(all_mask))
    first_products("B", (2, 3))
    if not segO:
        t.wait_ge(sem["qw2"], 1)
    second_product("A")
    first_products("H", range(HEAD))
    t.wait_ge(sem["v2"], 2 * count(all_mask))
    second_product("B")
    first_products("H", range(HEAD, G))
    second_product("H")

    if segO:
        tile_scalar("O")
        a, z = span(segO)
        s.wait_ge(sem["pO"], 1)
        s.activation(T.pO[:, a:z], bank("O", 4, a, z), ActivationFunctionType.Copy).then_inc(sem["evO"], 1)
        s.wait_ge(sem["hqO"], 1)
    tile_scalar("A")
    s.wait_ge(sem["pad"], 1)
    tile_scalar("B", *wantB)
    a, z = span(segA)
    s.wait_ge(sem["pA"], 1)
    s.activation(T.pA[:, a:z], bank("A", 4, a + base["A"], z + base["A"]),
                 ActivationFunctionType.Copy).then_inc(sem["evA"], 1)
    tile_scalar("H", *wantH)

    if wantB[1] != NC or not wantB[0]:
        raise ValueError("B's wanted columns end its tile")
    v.memset(T.hB[:, 0:4 * wantB[0]], 0.0).then_inc(sem["pad"], 1)
    if segO:
        tile_vector("O")
        pack("O")
        v.wait_ge(sem["hqO"], 1)
    tile_vector("A")
    pack("A")
    v.wait_ge(sem["pad"], 1)
    tile_vector("B", *wantB)
    pack("B")
    v.wait_ge(sem["gnear"], len(segB))
    v.wait_ge(sem["pB"], 1)
    a, z = span(segB)
    v.tensor_tensor(T.pB[:, a:z], bank("B", 4, a + base["B"], z + base["B"]), T.galn[:, a:z],
                    AluOpType.mult).then_inc(sem["evB"], 1)
    v.wait_ge(sem["hqA"], 1)
    tile_vector("H", *wantH)
    pack("H")

    v.wait_ge(sem["gown"], 1)

    def gated(out, src, segs, done):
        for a, z, row in segs:
            v.tensor_tensor(out[:, a:z], src(a, z), T.gall[:, NC * row + a:NC * row + z],
                            AluOpType.mult).then_inc(sem[done], 1)

    def summed(a, z, p, q):
        v.tensor_tensor(T.yb[:, a:z], p[:, a:z], q[:, a:z], AluOpType.add).then_inc(sem["ys"], 1)

    both = pieces(cnt, rank, lambda p, q: 0 if rank in (p, q) else None)
    half = pieces(cnt, rank, lambda p, q: 0 if on in (p, q) and rank not in (p, q) else None)
    gated(T.ho, lambda a, z: T.pO[:, a:z], segO, "hm")
    v.wait_ge(sem["pH"], 1)
    gated(T.ht, lambda a, z: bank("H", 4, a, z), segH, "hm")
    v.wait_ge(sem["ra"], count(off_mask))
    gated(T.ta, lambda a, z: T.ra[:, a:z], sendA, "tas")
    v.wait_ge(sem["hm"], len(segO) + len(segH))
    for a, z, _row in both:
        summed(a, z, T.ht, T.ho)
    v.wait_ge(sem["tas"], len(sendA))
    summed(*span(half), T.ta, T.ht)
    v.wait_ge(sem["rb"], count(off_mask))
    summed(*span(sendB), T.ta, T.rb)
    g.sync.wait_ge(sem["ys"], len(both) + 2)
    g.sync.dma_start(T.y[:], T.yb[:]).then_inc(sem["sty"], 16)
    g.sync.wait_ge(sem["sty"], 16)
    g.wait_ge(sem["sent"], sent[0])
